import numpy as np
import ml_dtypes


def mxq(x, axis, fmt="e4m3"):
    dtype, down = {"e4m3": (ml_dtypes.float8_e4m3fn, 7), "e5m2": (ml_dtypes.float8_e5m2, 14)}[fmt]
    v = np.moveaxis(np.asarray(x, np.float32).astype(ml_dtypes.bfloat16).astype(np.float64), axis, -1)
    blocks = v.reshape(v.shape[:-1] + (-1, 32))
    amax = np.abs(blocks).max(-1, keepdims=True)
    byte = np.maximum(np.where(amax > 0, np.frexp(amax)[1] - 1 + 127, 0) - down, 1)
    scale = np.exp2(byte - 127.0)
    codes = (blocks / scale).astype(np.float32).astype(dtype).astype(np.float64)
    return np.moveaxis((codes * scale).reshape(v.shape), -1, axis)


WIDE = False


def mx_kscale(k):
    if not WIDE:
        return np.ones(k)
    levels = np.array([10, -10, 5, -5, 0])
    if k % 512:
        return np.exp2(np.random.permutation(np.resize(levels, k // 32))).repeat(32)
    a = np.empty((k // 512, 16))
    for p in range(k // 512):
        a[p, :8] = np.random.permutation(np.resize(levels, 8))
        for g in range(8):
            far = levels[np.abs(levels - a[p, g]) >= 10]
            a[p, g + 8] = far[np.random.randint(len(far))]
    return np.exp2(a.ravel()).repeat(32)


def f64(x):
    return np.asarray(x).astype(np.float64)


def striped(idx):
    return np.tile(idx.reshape(-1, 16).T, (8, 1)).astype(np.uint16)


def unstriped(offs):
    return offs[:16].T.reshape(-1).astype(np.int64)


E2M1 = np.array([0.0, 0.5, 1.0, 1.5, 2.0, 3.0, 4.0, 6.0, -0.0, -0.5, -1.0, -1.5, -2.0, -3.0, -4.0, -6.0])


def pack_weight(w, fmt):
    k, n = w.shape
    w = f64(np.asarray(w, np.float32).astype(ml_dtypes.bfloat16)).reshape(k // 32, 32, n)
    amax = np.abs(w).max(1)
    if fmt == "e4m3":
        byte = np.frexp(amax)[1] - 1 + 127 - 7
    else:
        mant, ex = np.frexp(amax / 6.0)
        byte = np.where(mant > 0.5, ex, ex - 1) + 127
    byte = np.clip(np.where(amax > 0, byte, 1), 1, 254)
    scaled = (w * np.exp2(127.0 - byte)[:, None, :]).reshape(k, n).astype(np.float32)
    by_word = np.ascontiguousarray(scaled.reshape(k // 512, 128, 4, n).transpose(0, 1, 3, 2))
    if fmt == "e4m3":
        words = by_word.astype(ml_dtypes.float8_e4m3fn).view(np.uint8)
    else:
        c = by_word.astype(ml_dtypes.float4_e2m1fn).view(np.uint8) & 0xF
        words = (c[..., 0::2] | (c[..., 1::2] << 4)).reshape(k // 512, 128, 2 * n)
    return np.ascontiguousarray(words), np.ascontiguousarray(byte.astype(np.uint8).reshape(k // 512, 16, n))


def unpack_weight(words, scales, fmt):
    g, _, n = scales.shape
    words = np.ascontiguousarray(words).reshape(g, 128, n, -1)
    if fmt == "e4m3":
        vals = words.view(ml_dtypes.float8_e4m3fn).astype(np.float64)
    else:
        nib = np.empty((g, 128, n, 4), np.uint8)
        nib[..., 0::2] = words & 0xF
        nib[..., 1::2] = words >> 4
        vals = E2M1[nib]
    vals = vals * np.repeat(np.exp2(scales.astype(np.float64) - 127.0), 8, axis=1)[..., None]
    return vals.transpose(0, 1, 3, 2).reshape(g * 512, n)


def pack_table(v):
    words, scales = pack_weight(v, "e4m3")
    return np.concatenate([words.reshape(words.shape[0], -1), scales.reshape(scales.shape[0], -1)], axis=1)


def unpack_table(tab):
    g, t = tab.shape[0], tab.shape[1] // 528
    return unpack_weight(tab[:, :512 * t].reshape(g, 128, t, 4), tab[:, 512 * t:].reshape(g, 16, t), "e4m3")


def split(x):
    m, e = np.frexp(f64(x))
    hi = np.ldexp(np.trunc(16.0 * m) / 16.0, e)
    return hi, f64(x) - hi


def gelu(v):
    return 0.5 * v * (1.0 + np.tanh(np.sqrt(2.0 / np.pi) * (v + 0.044715 * v**3)))


K, M, T, S = 1024, 128, 2048, 512


def setup_inputs():
    n = np.random.standard_normal
    s = mx_kscale(K)[:, None]
    return {
        "tab": pack_table(n((K, T)) * s),
        "w": (n((K, M)) / np.sqrt(K) / s).astype(np.float32),
        "b": (0.3 * n(128)).astype(np.float32),
        "offs": striped(np.random.permutation(T)[:S]),
    }


def reference(tab, w, b, offs):
    tab_ = unpack_table(tab)[:, unstriped(offs)]
    w_hi, w_lo = split(w)
    w_hi_, w_lo_ = mxq(w_hi, 0, "e4m3"), mxq(w_lo, 0, "e4m3")
    y = tab_.T @ w_hi_ + tab_.T @ w_lo_
    return gelu(y + f64(b)[None, :])

@@ -1,0 +1,159 @@
+from contextlib import ExitStack
+
+import concourse.mybir as mybir
+
+K, N, T, S = 1024, 128, 2048, 512
+P = 128
+PASSES = 2
+PACK = 4
+GROUPS = S // P
+FLOPS = 2 * 2 * S * N * K
+
+F32 = mybir.dt.float32
+BF16 = mybir.dt.bfloat16
+I32 = mybir.dt.int32
+U32 = mybir.dt.uint32
+U16 = mybir.dt.uint16
+U8 = mybir.dt.uint8
+FP8X4 = mybir.dt.float8_e4m3fn_x4
+
+ALU = mybir.AluOpType
+GELU = mybir.ActivationFunctionType.Gelu_apprx_tanh
+HI_MASK = -983056
+
+
+def tile_list_tabw_tm_hl_gelu_kernel(tc, tab, w, b, offs, out):
+    nc = tc.nc
+    with ExitStack() as ctx:
+        keep = ctx.enter_context(tc.tile_pool(name="keep", bufs=1))
+        psum = ctx.enter_context(tc.psum_pool(name="psum", bufs=1))
+
+        offsets = keep.tile([P, S // 16], U16, name="offsets")
+        nc.sync.dma_start(offsets[:], offs)
+
+        bias_rows = keep.tile([P, N], F32, name="bias_rows", align_bytes=64)
+        nc.vector.memset(bias_rows[:], 0.0)
+        nc.sync.dma_start(out=bias_rows[0:P:32, :], in_=b.partition_broadcast(4))
+
+        table_scales = keep.tile([P, T // 4], I32, name="table_scales", tag="parts", align_bytes=64)
+        nc.vector.memset(table_scales[:], 0)
+        warm = keep.tile([P, 8], F32, name="warm")
+        warm_out = keep.tile([P, 8], F32, name="warm_out")
+        nc.vector.memset(warm[:], 0.0)
+        nc.scalar.activation(warm_out[:], warm[:], GELU)
+
+        w_raw = keep.tile([P, PASSES, PACK, N], F32, name="w_raw", align_bytes=64)
+        nc.sync.dma_start(out=w_raw[:], in_=w.rearrange("(a p j) n -> p a j n", p=P, j=PACK))
+        for q in range(4):
+            rows = tab[:, 512 * T + 4 * q * T : 512 * T + 4 * (q + 1) * T]
+            nc.sync.dma_start(
+                out=table_scales[32 * q : 32 * q + 8, :],
+                in_=rows.rearrange("a (r t) -> a r t", r=4).bitcast(I32),
+            )
+
+        table = [keep.tile([P, T], I32, name=f"table{a}", align_bytes=64) for a in range(PASSES)]
+        for a in range(PASSES):
+            nc.sync.dma_start(
+                out=table[a][:],
+                in_=tab[a, 0 : 512 * T].rearrange("(p x) -> p x", p=P).bitcast(I32),
+            )
+
+        bias_down = keep.tile([P, N], F32, name="bias_down", align_bytes=64)
+        bias_wide = keep.tile([P, N], F32, name="bias_wide", align_bytes=64)
+        bias = keep.tile([P, N], F32, name="bias", align_bytes=64)
+        nc.vector.transpose(bias_down[:], bias_rows[:])
+        nc.scalar.copy(
+            bias_wide[:].rearrange("p (c i) -> p c i", i=32),
+            bias_down[:].rearrange("p (c i) -> p c i", i=32)[:, :, 0:1].to_broadcast([P, 4, 32]),
+        )
+        picked_scales = keep.tile([P, S], U8, name="picked_scales", align_bytes=64)
+        nc.vector.tensor_copy(picked_scales[:], table_scales[:].bitcast(U8).indirect(offsets[:]))
+
+        cut = keep.tile([P, PASSES, N, PACK], BF16, name="cut", tag="cut", align_bytes=64)
+        parts = keep.tile([P, PASSES, 2, N, PACK], BF16, name="parts", tag="parts", align_bytes=64)
+        w_codes = [keep.tile([P, 2 * N], U32, name=f"w_codes{a}", align_bytes=64) for a in range(PASSES)]
+        w_scales = [keep.tile([P, 2 * N], U8, name=f"w_scales{a}", align_bytes=64) for a in range(PASSES)]
+        picked = []
+
+        def truncate(a):
+            halves = w_raw[:, a].bitcast(BF16).rearrange("p j (n h) -> p n j h", h=2)
+            nc.scalar.copy(cut[:, a], halves[:, :, :, 1])
+
+        def mask(a):
+            nc.vector.tensor_scalar(
+                out=parts[:, a, 0].rearrange("p n j -> p (n j)").bitcast(I32),
+                in0=cut[:, a].rearrange("p n j -> p (n j)").bitcast(I32),
+                scalar1=HI_MASK,
+                scalar2=None,
+                op0=ALU.bitwise_and,
+            )
+
+        def low(a, engine):
+            engine.tensor_tensor(
+                out=parts[:, a, 1],
+                in0=w_raw[:, a].rearrange("p j n -> p n j"),
+                in1=parts[:, a, 0],
+                op=ALU.subtract,
+            )
+
+        def quantize(a):
+            nc.vector.quantize_mx(
+                out=w_codes[a][:].bitcast(FP8X4),
+                scales=w_scales[a][:],
+                in_=parts[:, a].rearrange("p h n j -> p (h n j)"),
+            )
+
+        def gather(a, half):
+            nc.vector.tensor_copy(
+                picked[a][:, half * 256 : half * 256 + 256],
+                table[a][:].bitcast(U32).indirect(offsets[:, half * 16 : half * 16 + 16]),
+            )
+
+        truncate(0)
+        truncate(1)
+        mask(0)
+        mask(1)
+        low(0, nc.vector)
+        low(1, nc.vector)
+        quantize(0)
+        nc.vector.transpose(bias[:], bias_wide[:])
+        picked.append(keep.tile([P, S], U32, name="picked0", tag="cut", align_bytes=64))
+        gather(0, 0)
+        quantize(1)
+        gather(0, 1)
+        picked.append(keep.tile([P, S], U32, name="picked1", tag="parts", align_bytes=64))
+
+
+        sums = [psum.tile([P, N], F32, name=f"sums{g}") for g in range(GROUPS)]
+
+        def multiply(a, g):
+            toks = slice(g * P, g * P + P)
+            for h in range(2):
+                cols = slice(h * N, h * N + N)
+                nc.tensor.matmul_mx(
+                    out=sums[g][:],
+                    lhsT=picked[a][:, toks].bitcast(FP8X4),
+                    lhsT_scale=picked_scales[4 * a : P, toks],
+                    rhs=w_codes[a][:, cols].bitcast(FP8X4),
+                    rhs_scale=w_scales[a][:, cols],
+                    start=(a == 0 and h == 0),
+                    stop=(a == PASSES - 1 and h == 1),
+                )
+
+        for g in range(GROUPS):
+            multiply(0, g)
+
+        pre = keep.tile([P, GROUPS, N], F32, name="pre")
+        res = keep.tile([P, GROUPS, N], F32, name="res")
+        out_view = out.rearrange("(g p) n -> p g n", p=P)
+
+        gather(1, 0)
+        gather(1, 1)
+        for g in range(GROUPS):
+            multiply(1, g)
+            nc.vector.tensor_tensor(out=pre[:, g], in0=sums[g][:], in1=bias[:], op=ALU.add)
+            nc.scalar.activation(res[:, g], pre[:, g], GELU)
+            if g == 1:
+                nc.sync.dma_start(out=out_view[:, 0:2], in_=res[:, 0:2])
+            if g >= 2:
+                (nc.sync if g == 2 else nc.scalar).dma_start(out=out_view[:, g], in_=res[:, g])

@@ -1,6 +1,7 @@
 from contextlib import ExitStack
 
 import concourse.mybir as mybir
+from concourse.masks import make_identity
 
 K, N, T, S = 1024, 128, 2048, 512
 P = 128
@@ -31,9 +32,9 @@ def tile_list_tabw_tm_hl_gelu_kernel(tc, tab, w, b, offs, out):
         offsets = keep.tile([P, S // 16], U16, name="offsets")
         nc.sync.dma_start(offsets[:], offs)
 
-        bias_rows = keep.tile([P, N], F32, name="bias_rows", align_bytes=64)
-        nc.vector.memset(bias_rows[:], 0.0)
-        nc.sync.dma_start(out=bias_rows[0:P:32, :], in_=b.partition_broadcast(4))
+        bias_col = keep.tile([P, 1], F32, name="bias_col", align_bytes=64)
+        with nc.allow_non_contiguous_dma(reason="one bias value a partition"):
+            nc.scalar.dma_start(out=bias_col[:], in_=b.rearrange("(p o) -> p o", o=1))
 
         table_scales = keep.tile([P, T // 4], I32, name="table_scales", tag="parts", align_bytes=64)
         nc.vector.memset(table_scales[:], 0)
@@ -41,16 +42,17 @@ def tile_list_tabw_tm_hl_gelu_kernel(tc, tab, w, b, offs, out):
         warm_out = keep.tile([P, 8], F32, name="warm_out")
         nc.vector.memset(warm[:], 0.0)
         nc.scalar.activation(warm_out[:], warm[:], GELU)
+        identity = keep.tile([P, P], F32, name="identity", align_bytes=64)
+        nc.vector.memset(identity[:], 0.0)
+        make_identity(nc, identity[:], nomemset=True)
 
-        w_raw = keep.tile([P, PASSES, PACK, N], F32, name="w_raw", align_bytes=64)
-        nc.sync.dma_start(out=w_raw[:], in_=w.rearrange("(a p j) n -> p a j n", p=P, j=PACK))
-        for q in range(4):
-            rows = tab[:, 512 * T + 4 * q * T : 512 * T + 4 * (q + 1) * T]
-            nc.sync.dma_start(
-                out=table_scales[32 * q : 32 * q + 8, :],
-                in_=rows.rearrange("a (r t) -> a r t", r=4).bitcast(I32),
-            )
-
+        w_raw = [keep.tile([P, PACK, N], F32, name=f"w_raw{a}", align_bytes=64) for a in range(PASSES)]
+        w_rows = w.rearrange("(a p j) n -> a p j n", p=P, j=PACK)
+        nc.sync.dma_start(out=w_raw[0][:], in_=w_rows[0])
+        for a in range(PASSES):
+            rows = tab[a, 512 * T : 528 * T].rearrange("(q t) -> q t", q=16)
+            nc.sync.dma_start(out=table_scales[4 * a : P : 8, :], in_=rows.bitcast(I32))
+        nc.sync.dma_start(out=w_raw[1][:], in_=w_rows[1])
         table = [keep.tile([P, T], I32, name=f"table{a}", align_bytes=64) for a in range(PASSES)]
         for a in range(PASSES):
             nc.sync.dma_start(
@@ -58,16 +60,21 @@ def tile_list_tabw_tm_hl_gelu_kernel(tc, tab, w, b, offs, out):
                 in_=tab[a, 0 : 512 * T].rearrange("(p x) -> p x", p=P).bitcast(I32),
             )
 
-        bias_down = keep.tile([P, N], F32, name="bias_down", align_bytes=64)
-        bias_wide = keep.tile([P, N], F32, name="bias_wide", align_bytes=64)
+        bias_psum = psum.tile([P, N], F32, name="bias_psum")
         bias = keep.tile([P, N], F32, name="bias", align_bytes=64)
-        nc.vector.transpose(bias_down[:], bias_rows[:])
-        nc.scalar.copy(
-            bias_wide[:].rearrange("p (c i) -> p c i", i=32),
-            bias_down[:].rearrange("p (c i) -> p c i", i=32)[:, :, 0:1].to_broadcast([P, 4, 32]),
-        )
-        picked_scales = keep.tile([P, S], U8, name="picked_scales", align_bytes=64)
-        nc.vector.tensor_copy(picked_scales[:], table_scales[:].bitcast(U8).indirect(offsets[:]))
+        nc.tensor.transpose(bias_psum[:], bias_col[:].to_broadcast([P, P]), identity[:])
+        nc.scalar.copy(bias[:], bias_psum[:])
+        picked_rows = keep.tile([P, S], U8, name="picked_rows", align_bytes=64)
+        nc.vector.tensor_copy(picked_rows[:], table_scales[:].bitcast(U8).indirect(offsets[:]))
+        planes = keep.tile([P, S // 4], I32, name="planes", align_bytes=64)
+        nc.vector.tensor_copy(planes[:], picked_rows[:].bitcast(I32))
+        for a in range(PASSES):
+            for r in range(1, 4):
+                nc.scalar.dma_start(
+                    out=planes[4 * a + r : P : 32, :],
+                    in_=picked_rows[:].bitcast(I32)[8 * r + 4 * a : P : 32, :],
+                )
+        picked_scales = planes[:].bitcast(U8)
 
         cut = keep.tile([P, PASSES, N, PACK], BF16, name="cut", tag="cut", align_bytes=64)
         parts = keep.tile([P, PASSES, 2, N, PACK], BF16, name="parts", tag="parts", align_bytes=64)
@@ -76,7 +83,7 @@ def tile_list_tabw_tm_hl_gelu_kernel(tc, tab, w, b, offs, out):
         picked = []
 
         def truncate(a):
-            halves = w_raw[:, a].bitcast(BF16).rearrange("p j (n h) -> p n j h", h=2)
+            halves = w_raw[a][:].bitcast(BF16).rearrange("p j (n h) -> p n j h", h=2)
             nc.scalar.copy(cut[:, a], halves[:, :, :, 1])
 
         def mask(a):
@@ -91,7 +98,7 @@ def tile_list_tabw_tm_hl_gelu_kernel(tc, tab, w, b, offs, out):
         def low(a, engine):
             engine.tensor_tensor(
                 out=parts[:, a, 1],
-                in0=w_raw[:, a].rearrange("p j n -> p n j"),
+                in0=w_raw[a][:].rearrange("p j n -> p n j"),
                 in1=parts[:, a, 0],
                 op=ALU.subtract,
             )
@@ -116,7 +123,6 @@ def tile_list_tabw_tm_hl_gelu_kernel(tc, tab, w, b, offs, out):
         low(0, nc.vector)
         low(1, nc.vector)
         quantize(0)
-        nc.vector.transpose(bias[:], bias_wide[:])
         picked.append(keep.tile([P, S], U32, name="picked0", tag="cut", align_bytes=64))
         gather(0, 0)
         quantize(1)

@@ -20,7 +20,7 @@ FP8X4 = mybir.dt.float8_e4m3fn_x4
 
 ALU = mybir.AluOpType
 GELU = mybir.ActivationFunctionType.Gelu_apprx_tanh
-HI_MASK = -983056
+HI_MASK = -1048576
 
 
 def tile_list_tabw_tm_hl_gelu_kernel(tc, tab, w, b, offs, out):
@@ -36,8 +36,12 @@ def tile_list_tabw_tm_hl_gelu_kernel(tc, tab, w, b, offs, out):
         with nc.allow_non_contiguous_dma(reason="one bias value a partition"):
             nc.scalar.dma_start(out=bias_col[:], in_=b.rearrange("(p o) -> p o", o=1))
 
-        table_scales = keep.tile([P, T // 4], I32, name="table_scales", tag="parts", align_bytes=64)
-        nc.vector.memset(table_scales[:], 0)
+        table_scales = keep.tile([P, T // 4], I32, name="table_scales", align_bytes=64)
+        for a in range(PASSES):
+            rows = tab[a, 512 * T : 528 * T].rearrange("(q t) -> q t", q=16)
+            nc.sync.dma_start(out=table_scales[a:32:2, :], in_=rows.bitcast(I32))
+        nc.vector.memset(table_scales[32:64, :], 0)
+        nc.vector.memset(table_scales[64:P, :], 0)
         warm = keep.tile([P, 8], F32, name="warm")
         warm_out = keep.tile([P, 8], F32, name="warm_out")
         nc.vector.memset(warm[:], 0.0)
@@ -45,14 +49,12 @@ def tile_list_tabw_tm_hl_gelu_kernel(tc, tab, w, b, offs, out):
         identity = keep.tile([P, P], F32, name="identity", align_bytes=64)
         nc.vector.memset(identity[:], 0.0)
         make_identity(nc, identity[:], nomemset=True)
+        planes = keep.tile([P, PASSES * S // 4], I32, name="planes", align_bytes=64)
+        nc.vector.memset(planes[:], 0)
+        picked_scales = planes[:].bitcast(U8)
 
-        w_raw = [keep.tile([P, PACK, N], F32, name=f"w_raw{a}", align_bytes=64) for a in range(PASSES)]
-        w_rows = w.rearrange("(a p j) n -> a p j n", p=P, j=PACK)
-        nc.sync.dma_start(out=w_raw[0][:], in_=w_rows[0])
-        for a in range(PASSES):
-            rows = tab[a, 512 * T : 528 * T].rearrange("(q t) -> q t", q=16)
-            nc.sync.dma_start(out=table_scales[4 * a : P : 8, :], in_=rows.bitcast(I32))
-        nc.sync.dma_start(out=w_raw[1][:], in_=w_rows[1])
+        w_raw = keep.tile([P, PASSES, PACK, N], F32, name="w_raw", align_bytes=64)
+        nc.sync.dma_start(out=w_raw[:], in_=w.rearrange("(a p j) n -> p a j n", p=P, j=PACK))
         table = [keep.tile([P, T], I32, name=f"table{a}", align_bytes=64) for a in range(PASSES)]
         for a in range(PASSES):
             nc.sync.dma_start(
@@ -64,42 +66,36 @@ def tile_list_tabw_tm_hl_gelu_kernel(tc, tab, w, b, offs, out):
         bias = keep.tile([P, N], F32, name="bias", align_bytes=64)
         nc.tensor.transpose(bias_psum[:], bias_col[:].to_broadcast([P, P]), identity[:])
         nc.scalar.copy(bias[:], bias_psum[:])
+
         picked_rows = keep.tile([P, S], U8, name="picked_rows", align_bytes=64)
         nc.vector.tensor_copy(picked_rows[:], table_scales[:].bitcast(U8).indirect(offsets[:]))
-        planes = keep.tile([P, S // 4], I32, name="planes", align_bytes=64)
-        nc.vector.tensor_copy(planes[:], picked_rows[:].bitcast(I32))
-        for a in range(PASSES):
-            for r in range(1, 4):
-                nc.scalar.dma_start(
-                    out=planes[4 * a + r : P : 32, :],
-                    in_=picked_rows[:].bitcast(I32)[8 * r + 4 * a : P : 32, :],
-                )
-        picked_scales = planes[:].bitcast(U8)
+        for q in range(4):
+            nc.scalar.dma_start(
+                out=planes[32 * q : 32 * q + 4, :],
+                in_=picked_rows[:].bitcast(I32)[8 * q : 8 * q + 8, :],
+            )
 
-        cut = keep.tile([P, PASSES, N, PACK], BF16, name="cut", tag="cut", align_bytes=64)
+        high = keep.tile([P, PASSES, N, PACK], I32, name="high", align_bytes=64)
         parts = keep.tile([P, PASSES, 2, N, PACK], BF16, name="parts", tag="parts", align_bytes=64)
         w_codes = [keep.tile([P, 2 * N], U32, name=f"w_codes{a}", align_bytes=64) for a in range(PASSES)]
         w_scales = [keep.tile([P, 2 * N], U8, name=f"w_scales{a}", align_bytes=64) for a in range(PASSES)]
         picked = []
 
-        def truncate(a):
-            halves = w_raw[a][:].bitcast(BF16).rearrange("p j (n h) -> p n j h", h=2)
-            nc.scalar.copy(cut[:, a], halves[:, :, :, 1])
-
         def mask(a):
             nc.vector.tensor_scalar(
-                out=parts[:, a, 0].rearrange("p n j -> p (n j)").bitcast(I32),
-                in0=cut[:, a].rearrange("p n j -> p (n j)").bitcast(I32),
+                out=high[:, a],
+                in0=w_raw[:, a].bitcast(I32).rearrange("p j n -> p n j"),
                 scalar1=HI_MASK,
                 scalar2=None,
                 op0=ALU.bitwise_and,
             )
+            nc.scalar.copy(parts[:, a, 0], high[:, a].bitcast(F32))
 
-        def low(a, engine):
-            engine.tensor_tensor(
+        def low(a):
+            nc.vector.tensor_tensor(
                 out=parts[:, a, 1],
-                in0=w_raw[a][:].rearrange("p j n -> p n j"),
-                in1=parts[:, a, 0],
+                in0=w_raw[:, a].rearrange("p j n -> p n j"),
+                in1=high[:, a].bitcast(F32),
                 op=ALU.subtract,
             )
 
@@ -110,25 +106,21 @@ def tile_list_tabw_tm_hl_gelu_kernel(tc, tab, w, b, offs, out):
                 in_=parts[:, a].rearrange("p h n j -> p (h n j)"),
             )
 
-        def gather(a, half):
+        def gather(a, first, count):
             nc.vector.tensor_copy(
-                picked[a][:, half * 256 : half * 256 + 256],
-                table[a][:].bitcast(U32).indirect(offsets[:, half * 16 : half * 16 + 16]),
+                picked[a][:, first : first + count],
+                table[a][:].bitcast(U32).indirect(offsets[:, first // 16 : (first + count) // 16]),
             )
 
-        truncate(0)
-        truncate(1)
         mask(0)
         mask(1)
-        low(0, nc.vector)
-        low(1, nc.vector)
+        low(0)
+        low(1)
         quantize(0)
-        picked.append(keep.tile([P, S], U32, name="picked0", tag="cut", align_bytes=64))
-        gather(0, 0)
         quantize(1)
-        gather(0, 1)
+        picked.append(keep.tile([P, S], U32, name="picked0", align_bytes=64))
+        gather(0, 0, 512)
         picked.append(keep.tile([P, S], U32, name="picked1", tag="parts", align_bytes=64))
-
 
         sums = [psum.tile([P, N], F32, name=f"sums{g}") for g in range(GROUPS)]
 
@@ -139,7 +131,7 @@ def tile_list_tabw_tm_hl_gelu_kernel(tc, tab, w, b, offs, out):
                 nc.tensor.matmul_mx(
                     out=sums[g][:],
                     lhsT=picked[a][:, toks].bitcast(FP8X4),
-                    lhsT_scale=picked_scales[4 * a : P, toks],
+                    lhsT_scale=picked_scales[:, a * S + g * P : a * S + g * P + P],
                     rhs=w_codes[a][:, cols].bitcast(FP8X4),
                     rhs_scale=w_scales[a][:, cols],
                     start=(a == 0 and h == 0),
@@ -153,8 +145,8 @@ def tile_list_tabw_tm_hl_gelu_kernel(tc, tab, w, b, offs, out):
         res = keep.tile([P, GROUPS, N], F32, name="res")
         out_view = out.rearrange("(g p) n -> p g n", p=P)
 
-        gather(1, 0)
-        gather(1, 1)
+        gather(1, 0, 256)
+        gather(1, 256, 256)
         for g in range(GROUPS):
             multiply(1, g)
             nc.vector.tensor_tensor(out=pre[:, g], in0=sums[g][:], in1=bias[:], op=ALU.add)

@@ -60,6 +60,7 @@ def tile_list_tabw_tm_hl_gelu_kernel(tc, tab, w, b, offs, out):
             nc.sync.dma_start(
                 out=table[a][:],
                 in_=tab[a, 0 : 512 * T].rearrange("(p x) -> p x", p=P).bitcast(I32),
+                max_dma_last_dim=4096,
             )
 
         bias_psum = psum.tile([P, N], F32, name="bias_psum")
@@ -75,7 +76,7 @@ def tile_list_tabw_tm_hl_gelu_kernel(tc, tab, w, b, offs, out):
                 in_=picked_rows[:].bitcast(I32)[8 * q : 8 * q + 8, :],
             )
 
-        high = keep.tile([P, PASSES, N, PACK], I32, name="high", align_bytes=64)
+        high = keep.tile([P, PASSES, N, PACK], I32, name="high", tag="high", align_bytes=64)
         parts = keep.tile([P, PASSES, 2, N, PACK], BF16, name="parts", tag="parts", align_bytes=64)
         w_codes = [keep.tile([P, 2 * N], U32, name=f"w_codes{a}", align_bytes=64) for a in range(PASSES)]
         w_scales = [keep.tile([P, 2 * N], U8, name=f"w_scales{a}", align_bytes=64) for a in range(PASSES)]
@@ -117,9 +118,10 @@ def tile_list_tabw_tm_hl_gelu_kernel(tc, tab, w, b, offs, out):
         low(0)
         low(1)
         quantize(0)
+        picked.append(keep.tile([P, S], U32, name="picked0", tag="high", align_bytes=64))
+        gather(0, 0, 256)
+        gather(0, 256, 256)
         quantize(1)
-        picked.append(keep.tile([P, S], U32, name="picked0", align_bytes=64))
-        gather(0, 0, 512)
         picked.append(keep.tile([P, S], U32, name="picked1", tag="parts", align_bytes=64))
 
         sums = [psum.tile([P, N], F32, name=f"sums{g}") for g in range(GROUPS)]

@@ -36,22 +36,15 @@ def tile_list_tabw_tm_hl_gelu_kernel(tc, tab, w, b, offs, out):
         with nc.allow_non_contiguous_dma(reason="one bias value a partition"):
             nc.scalar.dma_start(out=bias_col[:], in_=b.rearrange("(p o) -> p o", o=1))
 
+        identity = keep.tile([P, P], F32, name="identity", align_bytes=64)
+        nc.vector.memset(identity[:], 0.0)
+        make_identity(nc, identity[:], nomemset=True)
         table_scales = keep.tile([P, T // 4], I32, name="table_scales", align_bytes=64)
         for a in range(PASSES):
             rows = tab[a, 512 * T : 528 * T].rearrange("(q t) -> q t", q=16)
             nc.sync.dma_start(out=table_scales[a:32:2, :], in_=rows.bitcast(I32))
         nc.vector.memset(table_scales[32:64, :], 0)
         nc.vector.memset(table_scales[64:P, :], 0)
-        warm = keep.tile([P, 8], F32, name="warm")
-        warm_out = keep.tile([P, 8], F32, name="warm_out")
-        nc.vector.memset(warm[:], 0.0)
-        nc.scalar.activation(warm_out[:], warm[:], GELU)
-        identity = keep.tile([P, P], F32, name="identity", align_bytes=64)
-        nc.vector.memset(identity[:], 0.0)
-        make_identity(nc, identity[:], nomemset=True)
-        planes = keep.tile([P, PASSES * S // 4], I32, name="planes", align_bytes=64)
-        nc.vector.memset(planes[:], 0)
-        picked_scales = planes[:].bitcast(U8)
 
         w_raw = keep.tile([P, PASSES, PACK, N], F32, name="w_raw", align_bytes=64)
         nc.sync.dma_start(out=w_raw[:], in_=w.rearrange("(a p j) n -> p a j n", p=P, j=PACK))
@@ -60,13 +53,15 @@ def tile_list_tabw_tm_hl_gelu_kernel(tc, tab, w, b, offs, out):
             nc.sync.dma_start(
                 out=table[a][:],
                 in_=tab[a, 0 : 512 * T].rearrange("(p x) -> p x", p=P).bitcast(I32),
-                max_dma_last_dim=4096,
             )
 
         bias_psum = psum.tile([P, N], F32, name="bias_psum")
         bias = keep.tile([P, N], F32, name="bias", align_bytes=64)
         nc.tensor.transpose(bias_psum[:], bias_col[:].to_broadcast([P, P]), identity[:])
         nc.scalar.copy(bias[:], bias_psum[:])
+        planes = keep.tile([P, PASSES * S // 4], I32, name="planes", tag="identity", align_bytes=64)
+        nc.gpsimd.memset(planes[:], 0)
+        picked_scales = planes[:].bitcast(U8)
 
         picked_rows = keep.tile([P, S], U8, name="picked_rows", align_bytes=64)
         nc.vector.tensor_copy(picked_rows[:], table_scales[:].bitcast(U8).indirect(offsets[:]))

@@ -7,6 +7,7 @@ K, N, T, S = 1024, 128, 2048, 512
 P = 128
 PASSES = 2
 PACK = 4
+LINE = 4
 GROUPS = S // P
 FLOPS = 2 * 2 * S * N * K
 
@@ -71,27 +72,33 @@ def tile_list_tabw_tm_hl_gelu_kernel(tc, tab, w, b, offs, out):
                 in_=picked_rows[:].bitcast(I32)[8 * q : 8 * q + 8, :],
             )
 
-        high = keep.tile([P, PASSES, N, PACK], I32, name="high", tag="high", align_bytes=64)
+        high = keep.tile([P, PASSES, PACK, N], I32, name="high", tag="high", align_bytes=64)
         parts = keep.tile([P, PASSES, 2, N, PACK], BF16, name="parts", tag="parts", align_bytes=64)
         w_codes = [keep.tile([P, 2 * N], U32, name=f"w_codes{a}", align_bytes=64) for a in range(PASSES)]
         w_scales = [keep.tile([P, 2 * N], U8, name=f"w_scales{a}", align_bytes=64) for a in range(PASSES)]
         picked = []
 
+        def by_lines(rows):
+            return rows.rearrange("p j (c i) -> p c j i", i=LINE)
+
+        def woven(words):
+            return words.rearrange("p (c i) j -> p c j i", i=LINE)
+
         def mask(a):
             nc.vector.tensor_scalar(
                 out=high[:, a],
-                in0=w_raw[:, a].bitcast(I32).rearrange("p j n -> p n j"),
+                in0=w_raw[:, a].bitcast(I32),
                 scalar1=HI_MASK,
                 scalar2=None,
                 op0=ALU.bitwise_and,
             )
-            nc.scalar.copy(parts[:, a, 0], high[:, a].bitcast(F32))
+            nc.scalar.copy(woven(parts[:, a, 0]), by_lines(high[:, a].bitcast(F32)))
 
         def low(a):
             nc.vector.tensor_tensor(
-                out=parts[:, a, 1],
-                in0=w_raw[:, a].rearrange("p j n -> p n j"),
-                in1=high[:, a].bitcast(F32),
+                out=woven(parts[:, a, 1]),
+                in0=by_lines(w_raw[:, a]),
+                in1=by_lines(high[:, a].bitcast(F32)),
                 op=ALU.subtract,
             )
 

@@ -33,17 +33,17 @@ def tile_list_tabw_tm_hl_gelu_kernel(tc, tab, w, b, offs, out):
         offsets = keep.tile([P, S // 16], U16, name="offsets")
         nc.sync.dma_start(offsets[:], offs)
 
-        bias_col = keep.tile([P, 1], F32, name="bias_col", align_bytes=64)
-        with nc.allow_non_contiguous_dma(reason="one bias value a partition"):
-            nc.scalar.dma_start(out=bias_col[:], in_=b.rearrange("(p o) -> p o", o=1))
+        bias_cols = keep.tile([P, LINE], F32, name="bias_cols", align_bytes=64)
+        nc.scalar.dma_start(out=bias_cols[0:32, :], in_=b.rearrange("(p j) -> p j", j=LINE))
+        nc.gpsimd.memset(bias_cols[32:64, :], 0.0)
+        nc.gpsimd.memset(bias_cols[64:P, :], 0.0)
 
         identity = keep.tile([P, P], F32, name="identity", align_bytes=64)
         nc.vector.memset(identity[:], 0.0)
         make_identity(nc, identity[:], nomemset=True)
         table_scales = keep.tile([P, T // 4], I32, name="table_scales", align_bytes=64)
-        for a in range(PASSES):
-            rows = tab[a, 512 * T : 528 * T].rearrange("(q t) -> q t", q=16)
-            nc.sync.dma_start(out=table_scales[a:32:2, :], in_=rows.bitcast(I32))
+        rows = tab[:, 512 * T : 528 * T].bitcast(I32).rearrange("a (q t) -> q a t", q=16)
+        nc.sync.dma_start(out=table_scales[0:32, :], in_=rows)
         nc.vector.memset(table_scales[32:64, :], 0)
         nc.vector.memset(table_scales[64:P, :], 0)
 
@@ -56,10 +56,14 @@ def tile_list_tabw_tm_hl_gelu_kernel(tc, tab, w, b, offs, out):
                 in_=tab[a, 0 : 512 * T].rearrange("(p x) -> p x", p=P).bitcast(I32),
             )
 
-        bias_psum = psum.tile([P, N], F32, name="bias_psum")
+        bias_psum = psum.tile([P, LINE, P], F32, name="bias_psum")
         bias = keep.tile([P, N], F32, name="bias", align_bytes=64)
-        nc.tensor.transpose(bias_psum[:], bias_col[:].to_broadcast([P, P]), identity[:])
-        nc.scalar.copy(bias[:], bias_psum[:])
+        for j in range(LINE):
+            nc.tensor.transpose(bias_psum[:, j], bias_cols[:, j : j + 1].to_broadcast([P, P]), identity[:])
+        nc.scalar.copy(
+            bias[:].rearrange("p (k j) -> p k j", j=LINE),
+            bias_psum[:, :, 0:32].rearrange("p j k -> p k j"),
+        )
         planes = keep.tile([P, PASSES * S // 4], I32, name="planes", tag="identity", align_bytes=64)
         nc.gpsimd.memset(planes[:], 0)
         picked_scales = planes[:].bitcast(U8)

@@ -34,7 +34,7 @@ def tile_list_tabw_tm_hl_gelu_kernel(tc, tab, w, b, offs, out):
         nc.sync.dma_start(offsets[:], offs)
 
         bias_cols = keep.tile([P, LINE], F32, name="bias_cols", align_bytes=64)
-        nc.scalar.dma_start(out=bias_cols[0:32, :], in_=b.rearrange("(p j) -> p j", j=LINE))
+        nc.sync.dma_start(out=bias_cols[0:32, :], in_=b.rearrange("(p j) -> p j", j=LINE))
         nc.gpsimd.memset(bias_cols[32:64, :], 0.0)
         nc.gpsimd.memset(bias_cols[64:P, :], 0.0)
 
@@ -43,15 +43,15 @@ def tile_list_tabw_tm_hl_gelu_kernel(tc, tab, w, b, offs, out):
         make_identity(nc, identity[:], nomemset=True)
         table_scales = keep.tile([P, T // 4], I32, name="table_scales", align_bytes=64)
         rows = tab[:, 512 * T : 528 * T].bitcast(I32).rearrange("a (q t) -> q a t", q=16)
-        nc.sync.dma_start(out=table_scales[0:32, :], in_=rows)
+        nc.scalar.dma_start(out=table_scales[0:32, :], in_=rows)
         nc.vector.memset(table_scales[32:64, :], 0)
         nc.vector.memset(table_scales[64:P, :], 0)
 
         w_raw = keep.tile([P, PASSES, PACK, N], F32, name="w_raw", align_bytes=64)
-        nc.sync.dma_start(out=w_raw[:], in_=w.rearrange("(a p j) n -> p a j n", p=P, j=PACK))
+        nc.scalar.dma_start(out=w_raw[:], in_=w.rearrange("(a p j) n -> p a j n", p=P, j=PACK))
         table = [keep.tile([P, T], I32, name=f"table{a}", align_bytes=64) for a in range(PASSES)]
         for a in range(PASSES):
-            nc.sync.dma_start(
+            nc.scalar.dma_start(
                 out=table[a][:],
                 in_=tab[a, 0 : 512 * T].rearrange("(p x) -> p x", p=P).bitcast(I32),
             )
@@ -64,14 +64,14 @@ def tile_list_tabw_tm_hl_gelu_kernel(tc, tab, w, b, offs, out):
             bias[:].rearrange("p (k j) -> p k j", j=LINE),
             bias_psum[:, :, 0:32].rearrange("p j k -> p k j"),
         )
-        planes = keep.tile([P, PASSES * S // 4], I32, name="planes", tag="identity", align_bytes=64)
+        planes = keep.tile([P, PASSES * S // 4], I32, name="planes", align_bytes=64)
         nc.gpsimd.memset(planes[:], 0)
         picked_scales = planes[:].bitcast(U8)
 
         picked_rows = keep.tile([P, S], U8, name="picked_rows", align_bytes=64)
         nc.vector.tensor_copy(picked_rows[:], table_scales[:].bitcast(U8).indirect(offsets[:]))
         for q in range(4):
-            nc.scalar.dma_start(
+            nc.sync.dma_start(
                 out=planes[32 * q : 32 * q + 4, :],
                 in_=picked_rows[:].bitcast(I32)[8 * q : 8 * q + 8, :],
             )

@@ -157,8 +157,11 @@ def tile_list_tabw_tm_hl_gelu_kernel(tc, tab, w, b, offs, out):
         gather(1, 256, 256)
         for g in range(GROUPS):
             multiply(1, g)
-            nc.vector.tensor_tensor(out=pre[:, g], in0=sums[g][:], in1=bias[:], op=ALU.add)
-            nc.scalar.activation(res[:, g], pre[:, g], GELU)
+            pieces = 2 if g == GROUPS - 1 else 1
+            for u in range(pieces):
+                cols = slice(u * N // pieces, (u + 1) * N // pieces)
+                nc.vector.tensor_tensor(out=pre[:, g, cols], in0=sums[g][:, cols], in1=bias[:, cols], op=ALU.add)
+                nc.scalar.activation(res[:, g, cols], pre[:, g, cols], GELU)
             if g == 1:
                 nc.sync.dma_start(out=out_view[:, 0:2], in_=res[:, 0:2])
             if g >= 2:

@@ -165,4 +165,4 @@ def tile_list_tabw_tm_hl_gelu_kernel(tc, tab, w, b, offs, out):
             if g == 1:
                 nc.sync.dma_start(out=out_view[:, 0:2], in_=res[:, 0:2])
             if g >= 2:
-                (nc.sync if g == 2 else nc.scalar).dma_start(out=out_view[:, g], in_=res[:, g])
+                nc.sync.dma_start(out=out_view[:, g], in_=res[:, g])

@@ -153,8 +153,8 @@ def tile_list_tabw_tm_hl_gelu_kernel(tc, tab, w, b, offs, out):
         res = keep.tile([P, GROUPS, N], F32, name="res")
         out_view = out.rearrange("(g p) n -> p g n", p=P)
 
-        gather(1, 0, 256)
-        gather(1, 256, 256)
+        for g in range(GROUPS):
+            gather(1, g * P, P)
         for g in range(GROUPS):
             multiply(1, g)
             pieces = 2 if g == GROUPS - 1 else 1

@@ -41,7 +41,7 @@ def tile_list_tabw_tm_hl_gelu_kernel(tc, tab, w, b, offs, out):
         identity = keep.tile([P, P], F32, name="identity", align_bytes=64)
         nc.vector.memset(identity[:], 0.0)
         make_identity(nc, identity[:], nomemset=True)
-        table_scales = keep.tile([P, T // 4], I32, name="table_scales", align_bytes=64)
+        table_scales = keep.tile([P, T // 4], I32, name="table_scales", tag="late", align_bytes=64)
         rows = tab[:, 512 * T : 528 * T].bitcast(I32).rearrange("a (q t) -> q a t", q=16)
         nc.scalar.dma_start(out=table_scales[0:32, :], in_=rows)
         nc.vector.memset(table_scales[32:64, :], 0)
@@ -49,21 +49,14 @@ def tile_list_tabw_tm_hl_gelu_kernel(tc, tab, w, b, offs, out):
 
         w_raw = keep.tile([P, PASSES, PACK, N], F32, name="w_raw", align_bytes=64)
         nc.scalar.dma_start(out=w_raw[:], in_=w.rearrange("(a p j) n -> p a j n", p=P, j=PACK))
-        table = [keep.tile([P, T], I32, name=f"table{a}", align_bytes=64) for a in range(PASSES)]
-        for a in range(PASSES):
-            nc.scalar.dma_start(
-                out=table[a][:],
-                in_=tab[a, 0 : 512 * T].rearrange("(p x) -> p x", p=P).bitcast(I32),
-            )
+        table = [keep.tile([P, T], I32, name="table0", align_bytes=64)]
+        nc.scalar.dma_start(out=table[0][:], in_=tab[0, 0 : 512 * T].rearrange("(p x) -> p x", p=P).bitcast(I32))
 
-        bias_psum = psum.tile([P, LINE, P], F32, name="bias_psum")
         bias = keep.tile([P, N], F32, name="bias", align_bytes=64)
         for j in range(LINE):
-            nc.tensor.transpose(bias_psum[:, j], bias_cols[:, j : j + 1].to_broadcast([P, P]), identity[:])
-        nc.scalar.copy(
-            bias[:].rearrange("p (k j) -> p k j", j=LINE),
-            bias_psum[:, :, 0:32].rearrange("p j k -> p k j"),
-        )
+            turned = psum.tile([P, P], F32, name=f"turned{j}", tag=f"bank{j}")
+            nc.tensor.transpose(turned[:], bias_cols[:, j : j + 1].to_broadcast([P, P]), identity[:])
+            nc.scalar.copy(bias[:].rearrange("p (k j) -> p j k", j=LINE)[:, j], turned[:, 0:32])
         planes = keep.tile([P, PASSES * S // 4], I32, name="planes", align_bytes=64)
         nc.gpsimd.memset(planes[:], 0)
         picked_scales = planes[:].bitcast(U8)
@@ -75,6 +68,8 @@ def tile_list_tabw_tm_hl_gelu_kernel(tc, tab, w, b, offs, out):
                 out=planes[32 * q : 32 * q + 4, :],
                 in_=picked_rows[:].bitcast(I32)[8 * q : 8 * q + 8, :],
             )
+        table.append(keep.tile([P, T], I32, name="table1", tag="late", align_bytes=64))
+        nc.sync.dma_start(out=table[1][:], in_=tab[1, 0 : 512 * T].rearrange("(p x) -> p x", p=P).bitcast(I32))
 
         high = keep.tile([P, PASSES, PACK, N], I32, name="high", tag="high", align_bytes=64)
         parts = keep.tile([P, PASSES, 2, N, PACK], BF16, name="parts", tag="parts", align_bytes=64)
@@ -130,7 +125,7 @@ def tile_list_tabw_tm_hl_gelu_kernel(tc, tab, w, b, offs, out):
         quantize(1)
         picked.append(keep.tile([P, S], U32, name="picked1", tag="parts", align_bytes=64))
 
-        sums = [psum.tile([P, N], F32, name=f"sums{g}") for g in range(GROUPS)]
+        sums = [psum.tile([P, N], F32, name=f"sums{g}", tag=f"bank{g}") for g in range(GROUPS)]
 
         def multiply(a, g):
             toks = slice(g * P, g * P + P)

@@ -41,7 +41,7 @@ def tile_list_tabw_tm_hl_gelu_kernel(tc, tab, w, b, offs, out):
         identity = keep.tile([P, P], F32, name="identity", align_bytes=64)
         nc.vector.memset(identity[:], 0.0)
         make_identity(nc, identity[:], nomemset=True)
-        table_scales = keep.tile([P, T // 4], I32, name="table_scales", tag="late", align_bytes=64)
+        table_scales = keep.tile([P, T // 4], I32, name="table_scales", align_bytes=64)
         rows = tab[:, 512 * T : 528 * T].bitcast(I32).rearrange("a (q t) -> q a t", q=16)
         nc.scalar.dma_start(out=table_scales[0:32, :], in_=rows)
         nc.vector.memset(table_scales[32:64, :], 0)
@@ -68,8 +68,8 @@ def tile_list_tabw_tm_hl_gelu_kernel(tc, tab, w, b, offs, out):
                 out=planes[32 * q : 32 * q + 4, :],
                 in_=picked_rows[:].bitcast(I32)[8 * q : 8 * q + 8, :],
             )
-        table.append(keep.tile([P, T], I32, name="table1", tag="late", align_bytes=64))
-        nc.sync.dma_start(out=table[1][:], in_=tab[1, 0 : 512 * T].rearrange("(p x) -> p x", p=P).bitcast(I32))
+        mask_word = keep.tile([P, 1], I32, name="mask_word", tag="late", align_bytes=64)
+        nc.gpsimd.memset(mask_word[:], HI_MASK)
 
         high = keep.tile([P, PASSES, PACK, N], I32, name="high", tag="high", align_bytes=64)
         parts = keep.tile([P, PASSES, 2, N, PACK], BF16, name="parts", tag="parts", align_bytes=64)
@@ -87,10 +87,12 @@ def tile_list_tabw_tm_hl_gelu_kernel(tc, tab, w, b, offs, out):
             nc.vector.tensor_scalar(
                 out=high[:, a],
                 in0=w_raw[:, a].bitcast(I32),
-                scalar1=HI_MASK,
+                scalar1=HI_MASK if a == 0 else mask_word[:],
                 scalar2=None,
                 op0=ALU.bitwise_and,
             )
+
+        def cast(a):
             nc.scalar.copy(woven(parts[:, a, 0]), by_lines(high[:, a].bitcast(F32)))
 
         def low(a):
@@ -116,6 +118,10 @@ def tile_list_tabw_tm_hl_gelu_kernel(tc, tab, w, b, offs, out):
 
         mask(0)
         mask(1)
+        table.append(keep.tile([P, T], I32, name="table1", tag="late", align_bytes=64))
+        nc.scalar.dma_start(out=table[1][:], in_=tab[1, 0 : 512 * T].rearrange("(p x) -> p x", p=P).bitcast(I32))
+        cast(0)
+        cast(1)
         low(0)
         low(1)
         quantize(0)

@@ -63,7 +63,7 @@ def tile_list_tabw_tm_hl_gelu_kernel(tc, tab, w, b, offs, out):
 
         picked_rows = keep.tile([P, S], U8, name="picked_rows", align_bytes=64)
         nc.vector.tensor_copy(picked_rows[:], table_scales[:].bitcast(U8).indirect(offsets[:]))
-        for q in range(4):
+        for q in (0, 2, 1, 3):
             nc.sync.dma_start(
                 out=planes[32 * q : 32 * q + 4, :],
                 in_=picked_rows[:].bitcast(I32)[8 * q : 8 * q + 8, :],
@@ -92,8 +92,8 @@ def tile_list_tabw_tm_hl_gelu_kernel(tc, tab, w, b, offs, out):
                 op0=ALU.bitwise_and,
             )
 
-        def cast(a):
-            nc.scalar.copy(woven(parts[:, a, 0]), by_lines(high[:, a].bitcast(F32)))
+        def cast(a, cols):
+            nc.scalar.copy(woven(parts[:, a, 0, cols]), by_lines(high[:, a].bitcast(F32)[:, :, cols]))
 
         def low(a):
             nc.vector.tensor_tensor(
@@ -117,11 +117,12 @@ def tile_list_tabw_tm_hl_gelu_kernel(tc, tab, w, b, offs, out):
             )
 
         mask(0)
+        cast(0, slice(0, 96))
         mask(1)
         table.append(keep.tile([P, T], I32, name="table1", tag="late", align_bytes=64))
         nc.scalar.dma_start(out=table[1][:], in_=tab[1, 0 : 512 * T].rearrange("(p x) -> p x", p=P).bitcast(I32))
-        cast(0)
-        cast(1)
+        cast(0, slice(96, N))
+        cast(1, slice(0, N))
         low(0)
         low(1)
         quantize(0)

@@ -34,18 +34,15 @@ def tile_list_tabw_tm_hl_gelu_kernel(tc, tab, w, b, offs, out):
         nc.sync.dma_start(offsets[:], offs)
 
         bias_cols = keep.tile([P, LINE], F32, name="bias_cols", align_bytes=64)
-        nc.sync.dma_start(out=bias_cols[0:32, :], in_=b.rearrange("(p j) -> p j", j=LINE))
-        nc.gpsimd.memset(bias_cols[32:64, :], 0.0)
-        nc.gpsimd.memset(bias_cols[64:P, :], 0.0)
+        nc.sync.dma_start(out=bias_cols[96:P, :], in_=b.rearrange("(p j) -> p j", j=LINE))
 
         identity = keep.tile([P, P], F32, name="identity", align_bytes=64)
-        nc.vector.memset(identity[:], 0.0)
-        make_identity(nc, identity[:], nomemset=True)
+        make_identity(nc, identity[:])
         table_scales = keep.tile([P, T // 4], I32, name="table_scales", align_bytes=64)
         rows = tab[:, 512 * T : 528 * T].bitcast(I32).rearrange("a (q t) -> q a t", q=16)
-        nc.scalar.dma_start(out=table_scales[0:32, :], in_=rows)
-        nc.vector.memset(table_scales[32:64, :], 0)
-        nc.vector.memset(table_scales[64:P, :], 0)
+        nc.scalar.dma_start(out=table_scales[96:P, :], in_=rows)
+        nc.vector.memset(table_scales[0:96, :], 0)
+        nc.vector.memset(bias_cols[0:96, :], 0.0)
 
         w_raw = keep.tile([P, PASSES, PACK, N], F32, name="w_raw", align_bytes=64)
         nc.scalar.dma_start(out=w_raw[:], in_=w.rearrange("(a p j) n -> p a j n", p=P, j=PACK))
@@ -56,9 +53,9 @@ def tile_list_tabw_tm_hl_gelu_kernel(tc, tab, w, b, offs, out):
         for j in range(LINE):
             turned = psum.tile([P, P], F32, name=f"turned{j}", tag=f"bank{j}")
             nc.tensor.transpose(turned[:], bias_cols[:, j : j + 1].to_broadcast([P, P]), identity[:])
-            nc.scalar.copy(bias[:].rearrange("p (k j) -> p j k", j=LINE)[:, j], turned[:, 0:32])
+            nc.scalar.copy(bias[:].rearrange("p (k j) -> p j k", j=LINE)[:, j], turned[:, 96:P])
         planes = keep.tile([P, PASSES * S // 4], I32, name="planes", align_bytes=64)
-        nc.gpsimd.memset(planes[:], 0)
+        nc.vector.memset(planes[:], 0)
         picked_scales = planes[:].bitcast(U8)
 
         picked_rows = keep.tile([P, S], U8, name="picked_rows", align_bytes=64)
@@ -66,10 +63,10 @@ def tile_list_tabw_tm_hl_gelu_kernel(tc, tab, w, b, offs, out):
         for q in (0, 2, 1, 3):
             nc.sync.dma_start(
                 out=planes[32 * q : 32 * q + 4, :],
-                in_=picked_rows[:].bitcast(I32)[8 * q : 8 * q + 8, :],
+                in_=picked_rows[:].bitcast(I32)[96 + 8 * q : 96 + 8 * q + 8, :],
             )
         mask_word = keep.tile([P, 1], I32, name="mask_word", tag="late", align_bytes=64)
-        nc.gpsimd.memset(mask_word[:], HI_MASK)
+        nc.vector.memset(mask_word[:], HI_MASK)
 
         high = keep.tile([P, PASSES, PACK, N], I32, name="high", tag="high", align_bytes=64)
         parts = keep.tile([P, PASSES, 2, N, PACK], BF16, name="parts", tag="parts", align_bytes=64)

@@ -68,8 +68,10 @@ def tile_list_tabw_tm_hl_gelu_kernel(tc, tab, w, b, offs, out):
         mask_word = keep.tile([P, 1], I32, name="mask_word", tag="late", align_bytes=64)
         nc.vector.memset(mask_word[:], HI_MASK)
 
-        high = keep.tile([P, PASSES, PACK, N], I32, name="high", tag="high", align_bytes=64)
-        parts = keep.tile([P, PASSES, 2, N, PACK], BF16, name="parts", tag="parts", align_bytes=64)
+        high = [keep.tile([P, PACK, N], I32, name=f"high{a}", tag=f"high{a}", align_bytes=64) for a in range(PASSES)]
+        parts = [
+            keep.tile([P, 2, N, PACK], BF16, name=f"parts{a}", tag=f"parts{a}", align_bytes=64) for a in range(PASSES)
+        ]
         w_codes = [keep.tile([P, 2 * N], U32, name=f"w_codes{a}", align_bytes=64) for a in range(PASSES)]
         w_scales = [keep.tile([P, 2 * N], U8, name=f"w_scales{a}", align_bytes=64) for a in range(PASSES)]
         picked = []
@@ -82,7 +84,7 @@ def tile_list_tabw_tm_hl_gelu_kernel(tc, tab, w, b, offs, out):
 
         def mask(a):
             nc.vector.tensor_scalar(
-                out=high[:, a],
+                out=high[a][:],
                 in0=w_raw[:, a].bitcast(I32),
                 scalar1=HI_MASK if a == 0 else mask_word[:],
                 scalar2=None,
@@ -90,13 +92,13 @@ def tile_list_tabw_tm_hl_gelu_kernel(tc, tab, w, b, offs, out):
             )
 
         def cast(a, cols):
-            nc.scalar.copy(woven(parts[:, a, 0, cols]), by_lines(high[:, a].bitcast(F32)[:, :, cols]))
+            nc.scalar.copy(woven(parts[a][:, 0, cols]), by_lines(high[a][:].bitcast(F32)[:, :, cols]))
 
         def low(a):
             nc.vector.tensor_tensor(
-                out=woven(parts[:, a, 1]),
+                out=woven(parts[a][:, 1]),
                 in0=by_lines(w_raw[:, a]),
-                in1=by_lines(high[:, a].bitcast(F32)),
+                in1=by_lines(high[a][:].bitcast(F32)),
                 op=ALU.subtract,
             )
 
@@ -104,7 +106,7 @@ def tile_list_tabw_tm_hl_gelu_kernel(tc, tab, w, b, offs, out):
             nc.vector.quantize_mx(
                 out=w_codes[a][:].bitcast(FP8X4),
                 scales=w_scales[a][:],
-                in_=parts[:, a].rearrange("p h n j -> p (h n j)"),
+                in_=parts[a][:].rearrange("p h n j -> p (h n j)"),
             )
 
         def gather(a, first, count):
@@ -123,11 +125,11 @@ def tile_list_tabw_tm_hl_gelu_kernel(tc, tab, w, b, offs, out):
         low(0)
         low(1)
         quantize(0)
-        picked.append(keep.tile([P, S], U32, name="picked0", tag="high", align_bytes=64))
+        picked.append(keep.tile([P, S], U32, name="picked0", tag="high1", align_bytes=64))
         gather(0, 0, 256)
         gather(0, 256, 256)
         quantize(1)
-        picked.append(keep.tile([P, S], U32, name="picked1", tag="parts", align_bytes=64))
+        picked.append(keep.tile([P, S], U32, name="picked1", align_bytes=64))
 
         sums = [psum.tile([P, N], F32, name=f"sums{g}", tag=f"bank{g}") for g in range(GROUPS)]
 

@@ -42,7 +42,8 @@ def tile_list_tabw_tm_hl_gelu_kernel(tc, tab, w, b, offs, out):
         rows = tab[:, 512 * T : 528 * T].bitcast(I32).rearrange("a (q t) -> q a t", q=16)
         nc.scalar.dma_start(out=table_scales[96:P, :], in_=rows)
         nc.vector.memset(table_scales[0:96, :], 0)
-        nc.vector.memset(bias_cols[0:96, :], 0.0)
+        nc.vector.memset(bias_cols[0:96, 0:2], 0.0)
+        nc.vector.tensor_copy(bias_cols[0:96, 2:LINE], bias_cols[0:96, 0:2])
 
         w_raw = keep.tile([P, PASSES, PACK, N], F32, name="w_raw", align_bytes=64)
         nc.scalar.dma_start(out=w_raw[:], in_=w.rearrange("(a p j) n -> p a j n", p=P, j=PACK))

@@ -126,10 +126,10 @@ def tile_list_tabw_tm_hl_gelu_kernel(tc, tab, w, b, offs, out):
         low(0)
         low(1)
         quantize(0)
+        quantize(1)
         picked.append(keep.tile([P, S], U32, name="picked0", tag="high1", align_bytes=64))
         gather(0, 0, 256)
         gather(0, 256, 256)
-        quantize(1)
         picked.append(keep.tile([P, S], U32, name="picked1", align_bytes=64))
 
         sums = [psum.tile([P, N], F32, name=f"sums{g}", tag=f"bank{g}") for g in range(GROUPS)]

@@ -117,11 +117,11 @@ def tile_list_tabw_tm_hl_gelu_kernel(tc, tab, w, b, offs, out):
             )
 
         mask(0)
-        cast(0, slice(0, 96))
+        cast(0, slice(0, 64))
         mask(1)
         table.append(keep.tile([P, T], I32, name="table1", tag="late", align_bytes=64))
         nc.scalar.dma_start(out=table[1][:], in_=tab[1, 0 : 512 * T].rearrange("(p x) -> p x", p=P).bitcast(I32))
-        cast(0, slice(96, N))
+        cast(0, slice(64, N))
         cast(1, slice(0, N))
         low(0)
         low(1)

@@ -48,7 +48,9 @@ def tile_list_tabw_tm_hl_gelu_kernel(tc, tab, w, b, offs, out):
         w_raw = keep.tile([P, PASSES, PACK, N], F32, name="w_raw", align_bytes=64)
         nc.scalar.dma_start(out=w_raw[:], in_=w.rearrange("(a p j) n -> p a j n", p=P, j=PACK))
         table = [keep.tile([P, T], I32, name="table0", align_bytes=64)]
-        nc.scalar.dma_start(out=table[0][:], in_=tab[0, 0 : 512 * T].rearrange("(p x) -> p x", p=P).bitcast(I32))
+        words0 = tab[0, 0 : 512 * T].rearrange("(p x) -> p x", p=P).bitcast(I32)
+        for first in range(2):
+            nc.scalar.dma_start(out=table[0][first:P:2, :], in_=words0[first:P:2, :])
 
         bias = keep.tile([P, N], F32, name="bias", align_bytes=64)
         for j in range(LINE):
@@ -164,7 +166,4 @@ def tile_list_tabw_tm_hl_gelu_kernel(tc, tab, w, b, offs, out):
                 cols = slice(u * N // pieces, (u + 1) * N // pieces)
                 nc.vector.tensor_tensor(out=pre[:, g, cols], in0=sums[g][:, cols], in1=bias[:, cols], op=ALU.add)
                 nc.scalar.activation(res[:, g, cols], pre[:, g, cols], GELU)
-            if g == 1:
-                nc.sync.dma_start(out=out_view[:, 0:2], in_=res[:, 0:2])
-            if g >= 2:
-                nc.sync.dma_start(out=out_view[:, g], in_=res[:, g])
+            nc.sync.dma_start(out=out_view[:, g], in_=res[:, g])

@@ -8,6 +8,7 @@ P = 128
 PASSES = 2
 PACK = 4
 LINE = 4
+PAIR = 2
 GROUPS = S // P
 FLOPS = 2 * 2 * S * N * K
 
@@ -80,10 +81,10 @@ def tile_list_tabw_tm_hl_gelu_kernel(tc, tab, w, b, offs, out):
         picked = []
 
         def by_lines(rows):
-            return rows.rearrange("p j (c i) -> p c j i", i=LINE)
+            return rows.rearrange("p j (c i) -> p c j i", i=PAIR)
 
         def woven(words):
-            return words.rearrange("p (c i) j -> p c j i", i=LINE)
+            return words.rearrange("p (c i) j -> p c j i", i=PAIR)
 
         def mask(a):
             nc.vector.tensor_scalar(

from contextlib import ExitStack

import concourse.mybir as mybir
from concourse.masks import make_identity

K, N, T, S = 1024, 128, 2048, 512
P = 128
PASSES = 2
PACK = 4
LINE = 4
PAIR = 2
GROUPS = S // P
FLOPS = 2 * 2 * S * N * K

F32 = mybir.dt.float32
BF16 = mybir.dt.bfloat16
I32 = mybir.dt.int32
U32 = mybir.dt.uint32
U16 = mybir.dt.uint16
U8 = mybir.dt.uint8
FP8X4 = mybir.dt.float8_e4m3fn_x4

ALU = mybir.AluOpType
GELU = mybir.ActivationFunctionType.Gelu_apprx_tanh
HI_MASK = -1048576


def tile_list_tabw_tm_hl_gelu_kernel(tc, tab, w, b, offs, out):
    nc = tc.nc
    with ExitStack() as ctx:
        keep = ctx.enter_context(tc.tile_pool(name="keep", bufs=1))
        psum = ctx.enter_context(tc.psum_pool(name="psum", bufs=1))

        offsets = keep.tile([P, S // 16], U16, name="offsets")
        nc.sync.dma_start(offsets[:], offs)

        bias_cols = keep.tile([P, LINE], F32, name="bias_cols", align_bytes=64)
        nc.sync.dma_start(out=bias_cols[96:P, :], in_=b.rearrange("(p j) -> p j", j=LINE))

        identity = keep.tile([P, P], F32, name="identity", align_bytes=64)
        make_identity(nc, identity[:])
        table_scales = keep.tile([P, T // 4], I32, name="table_scales", align_bytes=64)
        rows = tab[:, 512 * T : 528 * T].bitcast(I32).rearrange("a (q t) -> q a t", q=16)
        nc.scalar.dma_start(out=table_scales[96:P, :], in_=rows)
        nc.vector.memset(table_scales[0:96, :], 0)
        nc.vector.memset(bias_cols[0:96, 0:2], 0.0)
        nc.vector.tensor_copy(bias_cols[0:96, 2:LINE], bias_cols[0:96, 0:2])

        w_raw = keep.tile([P, PASSES, PACK, N], F32, name="w_raw", align_bytes=64)
        nc.scalar.dma_start(out=w_raw[:], in_=w.rearrange("(a p j) n -> p a j n", p=P, j=PACK))
        table = [keep.tile([P, T], I32, name="table0", align_bytes=64)]
        words0 = tab[0, 0 : 512 * T].rearrange("(p x) -> p x", p=P).bitcast(I32)
        for first in range(2):
            nc.scalar.dma_start(out=table[0][first:P:2, :], in_=words0[first:P:2, :])

        bias = keep.tile([P, N], F32, name="bias", align_bytes=64)
        for j in range(LINE):
            turned = psum.tile([P, P], F32, name=f"turned{j}", tag=f"bank{j}")
            nc.tensor.transpose(turned[:], bias_cols[:, j : j + 1].to_broadcast([P, P]), identity[:])
            nc.scalar.copy(bias[:].rearrange("p (k j) -> p j k", j=LINE)[:, j], turned[:, 96:P])
        planes = keep.tile([P, PASSES * S // 4], I32, name="planes", align_bytes=64)
        nc.vector.memset(planes[:], 0)
        picked_scales = planes[:].bitcast(U8)

        picked_rows = keep.tile([P, S], U8, name="picked_rows", align_bytes=64)
        nc.vector.tensor_copy(picked_rows[:], table_scales[:].bitcast(U8).indirect(offsets[:]))
        for q in (0, 2, 1, 3):
            nc.sync.dma_start(
                out=planes[32 * q : 32 * q + 4, :],
                in_=picked_rows[:].bitcast(I32)[96 + 8 * q : 96 + 8 * q + 8, :],
            )
        mask_word = keep.tile([P, 1], I32, name="mask_word", tag="late", align_bytes=64)
        nc.vector.memset(mask_word[:], HI_MASK)

        high = [keep.tile([P, PACK, N], I32, name=f"high{a}", tag=f"high{a}", align_bytes=64) for a in range(PASSES)]
        parts = [
            keep.tile([P, 2, N, PACK], BF16, name=f"parts{a}", tag=f"parts{a}", align_bytes=64) for a in range(PASSES)
        ]
        w_codes = [keep.tile([P, 2 * N], U32, name=f"w_codes{a}", align_bytes=64) for a in range(PASSES)]
        w_scales = [keep.tile([P, 2 * N], U8, name=f"w_scales{a}", align_bytes=64) for a in range(PASSES)]
        picked = []

        def by_lines(rows):
            return rows.rearrange("p j (c i) -> p c j i", i=PAIR)

        def woven(words):
            return words.rearrange("p (c i) j -> p c j i", i=PAIR)

        def mask(a):
            nc.vector.tensor_scalar(
                out=high[a][:],
                in0=w_raw[:, a].bitcast(I32),
                scalar1=HI_MASK if a == 0 else mask_word[:],
                scalar2=None,
                op0=ALU.bitwise_and,
            )

        def cast(a, cols):
            nc.scalar.copy(woven(parts[a][:, 0, cols]), by_lines(high[a][:].bitcast(F32)[:, :, cols]))

        def low(a):
            nc.vector.tensor_tensor(
                out=woven(parts[a][:, 1]),
                in0=by_lines(w_raw[:, a]),
                in1=by_lines(high[a][:].bitcast(F32)),
                op=ALU.subtract,
            )

        def quantize(a):
            nc.vector.quantize_mx(
                out=w_codes[a][:].bitcast(FP8X4),
                scales=w_scales[a][:],
                in_=parts[a][:].rearrange("p h n j -> p (h n j)"),
            )

        def gather(a, first, count):
            nc.vector.tensor_copy(
                picked[a][:, first : first + count],
                table[a][:].bitcast(U32).indirect(offsets[:, first // 16 : (first + count) // 16]),
            )

        mask(0)
        cast(0, slice(0, 64))
        mask(1)
        table.append(keep.tile([P, T], I32, name="table1", tag="late", align_bytes=64))
        nc.scalar.dma_start(out=table[1][:], in_=tab[1, 0 : 512 * T].rearrange("(p x) -> p x", p=P).bitcast(I32))
        cast(0, slice(64, N))
        cast(1, slice(0, N))
        low(0)
        low(1)
        quantize(0)
        quantize(1)
        picked.append(keep.tile([P, S], U32, name="picked0", tag="high1", align_bytes=64))
        gather(0, 0, 256)
        gather(0, 256, 256)
        picked.append(keep.tile([P, S], U32, name="picked1", align_bytes=64))

        sums = [psum.tile([P, N], F32, name=f"sums{g}", tag=f"bank{g}") for g in range(GROUPS)]

        def multiply(a, g):
            toks = slice(g * P, g * P + P)
            for h in range(2):
                cols = slice(h * N, h * N + N)
                nc.tensor.matmul_mx(
                    out=sums[g][:],
                    lhsT=picked[a][:, toks].bitcast(FP8X4),
                    lhsT_scale=picked_scales[:, a * S + g * P : a * S + g * P + P],
                    rhs=w_codes[a][:, cols].bitcast(FP8X4),
                    rhs_scale=w_scales[a][:, cols],
                    start=(a == 0 and h == 0),
                    stop=(a == PASSES - 1 and h == 1),
                )

        for g in range(GROUPS):
            multiply(0, g)

        pre = keep.tile([P, GROUPS, N], F32, name="pre")
        res = keep.tile([P, GROUPS, N], F32, name="res")
        out_view = out.rearrange("(g p) n -> p g n", p=P)

        for g in range(GROUPS):
            gather(1, g * P, P)
        for g in range(GROUPS):
            multiply(1, g)
            pieces = 2 if g == GROUPS - 1 else 1
            for u in range(pieces):
                cols = slice(u * N // pieces, (u + 1) * N // pieces)
                nc.vector.tensor_tensor(out=pre[:, g, cols], in0=sums[g][:, cols], in1=bias[:, cols], op=ALU.add)
                nc.scalar.activation(res[:, g, cols], pre[:, g, cols], GELU)
            nc.sync.dma_start(out=out_view[:, g], in_=res[:, g])
